import numpy as np
import ml_dtypes


def mxq(x, axis, fmt="e4m3"):
    dtype, down = {"e4m3": (ml_dtypes.float8_e4m3fn, 7), "e5m2": (ml_dtypes.float8_e5m2, 14)}[fmt]
    v = np.moveaxis(np.asarray(x, np.float32).astype(ml_dtypes.bfloat16).astype(np.float64), axis, -1)
    blocks = v.reshape(v.shape[:-1] + (-1, 32))
    amax = np.abs(blocks).max(-1, keepdims=True)
    byte = np.maximum(np.where(amax > 0, np.frexp(amax)[1] - 1 + 127, 0) - down, 1)
    scale = np.exp2(byte - 127.0)
    codes = (blocks / scale).astype(np.float32).astype(dtype).astype(np.float64)
    return np.moveaxis((codes * scale).reshape(v.shape), -1, axis)


WIDE = False


def mx_kscale(k):
    if not WIDE:
        return np.ones(k)
    levels = np.array([10, -10, 5, -5, 0])
    if k % 512:
        return np.exp2(np.random.permutation(np.resize(levels, k // 32))).repeat(32)
    a = np.empty((k // 512, 16))
    for p in range(k // 512):
        a[p, :8] = np.random.permutation(np.resize(levels, 8))
        for g in range(8):
            far = levels[np.abs(levels - a[p, g]) >= 10]
            a[p, g + 8] = far[np.random.randint(len(far))]
    return np.exp2(a.ravel()).repeat(32)


BF16 = ml_dtypes.bfloat16


def bf(x):
    return np.asarray(x, np.float32).astype(BF16)


def f64(x):
    return np.asarray(x).astype(np.float64)

def planes(Y):
    n, m = Y.shape
    b = f64(bf(Y)).reshape(n // 32, 32, m)
    amax = np.abs(b).max(1)
    byte = np.clip(np.where(amax > 0, np.frexp(amax)[1] - 1 + 127 - 7, 1), 1, 254)
    codes = (b * np.exp2(127.0 - byte)[:, None, :]).reshape(n, m).astype(np.float32).astype(ml_dtypes.float8_e4m3fn).view(np.uint8)
    words = codes.reshape(n // 512, 128, 4, m).transpose(0, 1, 3, 2)
    return np.ascontiguousarray(words), np.ascontiguousarray(byte.astype(np.uint8).reshape(n // 512, 16, m))


T, SLOTS, WIDTH = 1024, 2048, 1024


def setup_inputs():
    s = mx_kscale(T)
    spread = np.exp(0.7 * np.random.randn(SLOTS))
    addr = np.random.randn(T, SLOTS) * spread[None, :]
    content = np.random.randn(T, WIDTH) / np.sqrt(T)
    retain = 0.5 * np.random.randn(T, WIDTH) / np.sqrt(T)
    memory = np.random.randn(SLOTS, WIDTH) * spread[:, None]
    bias = 0.5 * np.random.randn(SLOTS)
    return {
        "addr": bf(addr * s[:, None]),
        "content": bf(content / s[:, None]),
        "retain": bf(retain / s[:, None]),
        "memory": bf(memory),
        "bias": bf(bias),
    }

def reference(addr, content, retain, memory, bias):
    a = mxq(f64(addr), 0, "e4m3")
    c = mxq(f64(content), 0, "e4m3")
    r = mxq(f64(retain), 0, "e4m3")
    write = a.T @ c
    logit = a.T @ r
    keep = 1.0 / (1.0 + np.exp(-(logit + f64(bias)[:, None])))
    y = f64(memory) * keep + write
    Y = y.reshape(SLOTS, WIDTH)
    words, scales = planes(Y)
    return y, words, scales

@@ -1,0 +1,217 @@
+from contextlib import ExitStack
+
+import concourse.mybir as mybir
+
+T, SLOTS, WIDTH = 1024, 2048, 1024
+FLOPS = 2 * 2 * T * SLOTS * WIDTH
+
+F32 = mybir.dt.float32
+BF16 = mybir.dt.bfloat16
+I32 = mybir.dt.int32
+U32 = mybir.dt.uint32
+U8 = mybir.dt.uint8
+FP8X4 = mybir.dt.float8_e4m3fn_x4
+ACT = mybir.ActivationFunctionType
+ALU = mybir.AluOpType
+
+P = 128
+PACK = 4
+KP = P * PACK
+PASSES = T // KP
+GROUPS = SLOTS // KP
+N = 512
+HALVES = WIDTH // N
+STEPS = GROUPS * HALVES * PACK
+V_COLS = 256
+PIECE = 128
+
+
+def tile_gated_memory_write_g2_kernel(tc, addr, content, retain, memory, bias, out_0, out_1, out_2):
+    nc = tc.nc
+    with ExitStack() as ctx:
+        keep_pool = ctx.enter_context(tc.tile_pool(name="resident", bufs=1))
+        stage = ctx.enter_context(tc.tile_pool(name="stage", bufs=3))
+        ystage = ctx.enter_context(tc.tile_pool(name="ystage", bufs=2))
+        psum = ctx.enter_context(tc.psum_pool(name="psum", bufs=4))
+        ctx.enter_context(tc.manual_schedule())
+
+        source = {"a": addr, "c": content, "r": retain}
+        raw, codes, scales = {}, {}, {}
+        for op in "rac":
+            width = source[op].shape[1]
+            for k in range(PASSES):
+                codes[op, k] = keep_pool.tile([P, width], U32, name="codes_%s%d" % (op, k), align_bytes=64)
+                scales[op, k] = keep_pool.tile([P, width], U8, name="scales_%s%d" % (op, k), align_bytes=64)
+        mem = [keep_pool.tile([P, PACK, WIDTH], BF16, name="mem%d" % g, align_bytes=64) for g in range(GROUPS)]
+        y_codes = [keep_pool.tile([P, WIDTH], U32, name="y_codes%d" % g, align_bytes=64) for g in range(GROUPS)]
+        y_scales = keep_pool.tile([P, WIDTH], U8, name="y_scales", align_bytes=64)
+        bias_sb = keep_pool.tile([P, GROUPS, PACK], BF16, name="bias_sb", align_bytes=64)
+        warm_in = keep_pool.tile([P, 1], F32, name="warm_in")
+        warm_out = keep_pool.tile([P, 1], F32, name="warm_out")
+
+        def load(op, k, c0, c1):
+            rows = source[op][k * KP:(k + 1) * KP, c0 * N:c1 * N]
+            dst = keep_pool.tile([P, PACK, (c1 - c0) * N], BF16, name="raw_%s%d%d" % (op, k, c0), align_bytes=64)
+            nc.sync.dma_start(out=dst[:], in_=rows.rearrange("(p j) w -> p j w", j=PACK))
+            for c in range(c0, c1):
+                raw[op, k, c] = dst[:, :, (c - c0) * N:(c - c0 + 1) * N]
+
+        def load_mem(g, t0, t1):
+            rows = memory[g * KP:(g + 1) * KP, :].rearrange("(p t) w -> p t w", t=PACK)
+            nc.sync.dma_start(out=mem[g][:, t0:t1, :], in_=rows[:, t0:t1, :])
+
+        nc.vector.memset(warm_in[:], 0.0)
+        nc.scalar.activation(out=warm_out[:], in_=warm_in[:], func=ACT.Sigmoid)
+
+        load("r", 0, 0, 1)
+        load("r", 0, 1, 2)
+        load("a", 0, 0, 1)
+        load("r", 1, 0, 2)
+        load("a", 1, 0, 1)
+        nc.sync.dma_start(out=bias_sb[:], in_=bias.rearrange("(g p t) -> p g t", p=P, t=PACK))
+        load("c", 0, 0, 2)
+        load_mem(0, 0, 2)
+        load("c", 1, 0, 2)
+        load_mem(0, 2, 4)
+        load("a", 0, 1, 2)
+        load("a", 1, 1, 2)
+        load_mem(1, 0, 4)
+        load("a", 0, 2, 4)
+        load("a", 1, 2, 4)
+        load_mem(2, 0, 4)
+        load_mem(3, 0, 4)
+
+        grouped = {}
+
+        def interleave(chunk):
+            op, k, c = chunk
+            dst = stage.tile([P, N * PACK], BF16, name="grouped", align_bytes=64)
+            grouped[chunk] = dst
+            src = raw[chunk]
+            if op == "a":
+                src4 = src.rearrange("p j (m t) -> p m j t", t=PACK)
+                dst4 = dst[:].rearrange("p (t m j) -> p m j t", t=PACK, j=PACK)
+                nc.vector.tensor_copy(out=dst4[:, :, :, :2], in_=src4[:, :, :, :2])
+                nc.scalar.copy(out=dst4[:, :, :, 2:], in_=src4[:, :, :, 2:])
+            else:
+                src4 = src.rearrange("p j (c i) -> p c j i", i=PACK)
+                dst4 = dst[:].rearrange("p (c i j) -> p c j i", i=PACK, j=PACK)
+                cut = V_COLS // PACK
+                nc.vector.tensor_copy(out=dst4[:, :cut], in_=src4[:, :cut])
+                nc.scalar.copy(out=dst4[:, cut:], in_=src4[:, cut:])
+
+        def quantize(chunk):
+            op, k, c = chunk
+            cols = slice(c * N, (c + 1) * N)
+            nc.vector.quantize_mx(out=codes[op, k][:, cols].bitcast(FP8X4), scales=scales[op, k][:, cols], in_=grouped[chunk][:])
+
+        def where(s):
+            return s // (HALVES * PACK), (s // PACK) % HALVES, s % PACK
+
+        banks = {}
+
+        def product(op, s):
+            g, h, t = where(s)
+            bank = psum.tile([P, N], F32, name="bank_" + op)
+            banks[op, s] = bank
+            slots = slice(g * KP + t * P, g * KP + (t + 1) * P)
+            cols = slice(h * N, (h + 1) * N)
+            for k in range(PASSES):
+                nc.tensor.matmul_mx(out=bank[:], lhsT=codes["a", k][:, slots].bitcast(FP8X4), lhsT_scale=scales["a", k][:, slots],
+                                    rhs=codes[op, k][:, cols].bitcast(FP8X4), rhs_scale=scales[op, k][:, cols],
+                                    start=(k == 0), stop=(k == PASSES - 1))
+
+        gates, ys, y_bf = {}, {}, {}
+
+        def gate(s):
+            g, h, t = where(s)
+            keep = stage.tile([P, N], F32, name="keep")
+            gates[s] = keep
+            nc.scalar.activation(out=keep[:], in_=banks["r", s][:], func=ACT.Sigmoid, bias=bias_sb[:, g, t:t + 1])
+
+        def retain_memory(s):
+            g, h, t = where(s)
+            if t == 0:
+                ys[g, h] = ystage.tile([P, PACK, N], F32, name="y", bufs=6)
+            nc.vector.tensor_tensor(out=ys[g, h][:, t, :], in0=gates[s][:], in1=mem[g][:, t, h * N:(h + 1) * N], op=ALU.mult)
+
+        def add_write(s):
+            g, h, t = where(s)
+            nc.vector.tensor_tensor(out=ys[g, h][:, t, :], in0=banks["c", s][:], in1=ys[g, h][:, t, :], op=ALU.add)
+
+        def round_y(u, m0, m1, copy):
+            g, h = divmod(u, HALVES)
+            if u not in y_bf:
+                y_bf[u] = ystage.tile([P, N * PACK], BF16, name="y_bf", align_bytes=64)
+            src = ys[g, h][:, :, m0:m1].rearrange("p t (c i) -> p c t i", i=PACK)
+            dst = y_bf[u][:, m0 * PACK:m1 * PACK].rearrange("p (c i t) -> p c t i", i=PACK, t=PACK)
+            copy(out=dst, in_=src)
+
+        def quantize_y(u):
+            g, h = divmod(u, HALVES)
+            cols = slice(h * N, (h + 1) * N)
+            nc.vector.quantize_mx(out=y_codes[g][:, cols].bitcast(FP8X4), scales=y_scales[PACK * g:, cols], in_=y_bf[u][:])
+
+        def store_y(g, h, t0, t1):
+            rows = out_0[g * KP:(g + 1) * KP, :].rearrange("(p t) m -> p t m", t=PACK)
+            nc.sync.dma_start(out=rows[:, t0:t1, h * N:(h + 1) * N], in_=ys[g, h][:, t0:t1, :])
+
+        def store_words(g, c0, c1):
+            words = out_1[g].rearrange("p m t -> p (m t)").bitcast(I32)
+            nc.sync.dma_start(out=words[:, c0:c1], in_=y_codes[g][:, c0:c1].bitcast(I32))
+
+        head = [("r", 0, 0), ("r", 0, 1), ("a", 0, 0), ("r", 1, 0), ("r", 1, 1), ("a", 1, 0),
+                ("c", 0, 0), ("c", 0, 1), ("c", 1, 0), ("c", 1, 1)]
+        chunk_at = dict(enumerate(head))
+        chunk_at.update({11: ("a", 0, 1), 12: ("a", 1, 1), 16: ("a", 0, 2), 18: ("a", 1, 2), 23: ("a", 0, 3), 25: ("a", 1, 3)})
+        last_unit = GROUPS * HALVES - 1
+        for tick in range(STEPS + 11):
+            if 0 <= tick - 7 < STEPS:
+                gate(tick - 7)
+            if 0 <= tick - 8 < STEPS:
+                retain_memory(tick - 8)
+            if tick in chunk_at:
+                interleave(chunk_at[tick])
+            s = tick - 10
+            if 0 <= s < STEPS:
+                add_write(s)
+                g, h, t = where(s)
+                if s // PACK == last_unit:
+                    store_y(g, h, t, t + 1)
+                elif t == PACK - 1:
+                    store_y(g, h, 0, PACK)
+            if tick - 1 in chunk_at:
+                quantize(chunk_at[tick - 1])
+            if tick >= 18 and (tick - 18) % PACK == 0:
+                u = (tick - 18) // PACK
+                quantize_y(u)
+                if u % HALVES == 1:
+                    store_words(u // HALVES, 0, WIDTH)
+                elif u == last_unit - 1:
+                    store_words(u // HALVES, 0, N)
+            if tick >= 14:
+                u, q = divmod(tick - 14, PACK)
+                if u < last_unit:
+                    round_y(u, q * PIECE, (q + 1) * PIECE, nc.scalar.copy)
+            if tick == 6:
+                for s in range(2):
+                    product("r", s)
+            if tick == 7:
+                for s in range(2, 3):
+                    product("r", s)
+            if tick == 9:
+                for s in range(2):
+                    product("c", s)
+            if tick >= 10 and tick - 8 < STEPS:
+                product("c", tick - 8)
+            if tick >= 8 and tick - 5 < STEPS:
+                product("r", tick - 5)
+
+        round_y(last_unit, 0, 192, nc.scalar.copy)
+        round_y(last_unit, 192, N, nc.vector.tensor_copy)
+        quantize_y(last_unit)
+        store_words(GROUPS - 1, N, WIDTH)
+        for q in range(PACK):
+            queue = nc.sync if q % 2 == 0 else nc.scalar
+            queue.dma_start(out=out_2[:, PACK * q:PACK * (q + 1), :].bitcast(I32),
+                            in_=y_scales[32 * q:32 * q + PACK * GROUPS, :].bitcast(I32))

@@ -22,8 +22,8 @@ GROUPS = SLOTS // KP
 N = 512
 HALVES = WIDTH // N
 STEPS = GROUPS * HALVES * PACK
-V_COLS = 256
-PIECE = 128
+V_COLS = 224
+G_COLS = 0
 
 
 def tile_gated_memory_write_g2_kernel(tc, addr, content, retain, memory, bias, out_0, out_1, out_2):
@@ -42,7 +42,7 @@ def tile_gated_memory_write_g2_kernel(tc, addr, content, retain, memory, bias, o
             for k in range(PASSES):
                 codes[op, k] = keep_pool.tile([P, width], U32, name="codes_%s%d" % (op, k), align_bytes=64)
                 scales[op, k] = keep_pool.tile([P, width], U8, name="scales_%s%d" % (op, k), align_bytes=64)
-        mem = [keep_pool.tile([P, PACK, WIDTH], BF16, name="mem%d" % g, align_bytes=64) for g in range(GROUPS)]
+        mem = {}
         y_codes = [keep_pool.tile([P, WIDTH], U32, name="y_codes%d" % g, align_bytes=64) for g in range(GROUPS)]
         y_scales = keep_pool.tile([P, WIDTH], U8, name="y_scales", align_bytes=64)
         bias_sb = keep_pool.tile([P, GROUPS, PACK], BF16, name="bias_sb", align_bytes=64)
@@ -56,162 +56,233 @@ def tile_gated_memory_write_g2_kernel(tc, addr, content, retain, memory, bias, o
             for c in range(c0, c1):
                 raw[op, k, c] = dst[:, :, (c - c0) * N:(c - c0 + 1) * N]
 
-        def load_mem(g, t0, t1):
-            rows = memory[g * KP:(g + 1) * KP, :].rearrange("(p t) w -> p t w", t=PACK)
-            nc.sync.dma_start(out=mem[g][:, t0:t1, :], in_=rows[:, t0:t1, :])
+        def load_mem(g, h0, h1):
+            rows = memory[g * KP:(g + 1) * KP, h0 * N:h1 * N]
+            dst = keep_pool.tile([P, PACK, (h1 - h0) * N], BF16, name="mem%d%d" % (g, h0), align_bytes=64)
+            nc.sync.dma_start(out=dst[:], in_=rows.rearrange("(p t) w -> p t w", t=PACK))
+            for h in range(h0, h1):
+                mem[g, h] = dst[:, :, (h - h0) * N:(h - h0 + 1) * N]
 
         nc.vector.memset(warm_in[:], 0.0)
         nc.scalar.activation(out=warm_out[:], in_=warm_in[:], func=ACT.Sigmoid)
 
         load("r", 0, 0, 1)
-        load("r", 0, 1, 2)
         load("a", 0, 0, 1)
-        load("r", 1, 0, 2)
+        load("r", 1, 0, 1)
         load("a", 1, 0, 1)
+        load("c", 0, 0, 1)
+        load("c", 1, 0, 1)
         nc.sync.dma_start(out=bias_sb[:], in_=bias.rearrange("(g p t) -> p g t", p=P, t=PACK))
-        load("c", 0, 0, 2)
-        load_mem(0, 0, 2)
-        load("c", 1, 0, 2)
-        load_mem(0, 2, 4)
+        load_mem(0, 0, 1)
+        load("r", 0, 1, 2)
+        load("r", 1, 1, 2)
+        load("c", 0, 1, 2)
+        load("c", 1, 1, 2)
+        load_mem(0, 1, 2)
         load("a", 0, 1, 2)
         load("a", 1, 1, 2)
-        load_mem(1, 0, 4)
+        load_mem(1, 0, 2)
         load("a", 0, 2, 4)
         load("a", 1, 2, 4)
-        load_mem(2, 0, 4)
-        load_mem(3, 0, 4)
+        load_mem(2, 0, 2)
+        load_mem(3, 0, 2)
 
         grouped = {}
 
-        def interleave(chunk):
+        def interleave(chunk, half, copy):
             op, k, c = chunk
-            dst = stage.tile([P, N * PACK], BF16, name="grouped", align_bytes=64)
-            grouped[chunk] = dst
-            src = raw[chunk]
+            if chunk not in grouped:
+                grouped[chunk] = stage.tile([P, N * PACK], BF16, name="grouped", align_bytes=64)
+            src, dst = raw[chunk], grouped[chunk][:]
             if op == "a":
-                src4 = src.rearrange("p j (m t) -> p m j t", t=PACK)
-                dst4 = dst[:].rearrange("p (t m j) -> p m j t", t=PACK, j=PACK)
-                nc.vector.tensor_copy(out=dst4[:, :, :, :2], in_=src4[:, :, :, :2])
-                nc.scalar.copy(out=dst4[:, :, :, 2:], in_=src4[:, :, :, 2:])
+                part = slice(2 * half, 2 * half + 2)
+                copy(out=dst.rearrange("p (t m j) -> p m j t", t=PACK, j=PACK)[:, :, :, part],
+                     in_=src.rearrange("p j (m t) -> p m j t", t=PACK)[:, :, :, part])
             else:
-                src4 = src.rearrange("p j (c i) -> p c j i", i=PACK)
-                dst4 = dst[:].rearrange("p (c i j) -> p c j i", i=PACK, j=PACK)
-                cut = V_COLS // PACK
-                nc.vector.tensor_copy(out=dst4[:, :cut], in_=src4[:, :cut])
-                nc.scalar.copy(out=dst4[:, cut:], in_=src4[:, cut:])
+                cut = (V_COLS if c else N // 2) // PACK
+                part = slice(cut, N // PACK) if half else slice(0, cut)
+                copy(out=dst.rearrange("p (c i j) -> p c j i", i=PACK, j=PACK)[:, part],
+                     in_=src.rearrange("p j (c i) -> p c j i", i=PACK)[:, part])
 
         def quantize(chunk):
             op, k, c = chunk
             cols = slice(c * N, (c + 1) * N)
             nc.vector.quantize_mx(out=codes[op, k][:, cols].bitcast(FP8X4), scales=scales[op, k][:, cols], in_=grouped[chunk][:])
 
-        def where(s):
-            return s // (HALVES * PACK), (s // PACK) % HALVES, s % PACK
+        units = [(g, h * N, N) for g in range(GROUPS) for h in range(HALVES)][:-1] + [(3, 512, 256), (3, 768, 256)]
+        last = len(units) - 1
+        banks, gates, ys, y_bf = {}, {}, {}, {}
 
-        banks = {}
+        def rows_of(u, b):
+            per_bank = N // units[u][2]
+            return range(b * per_bank, (b + 1) * per_bank)
 
-        def product(op, s):
-            g, h, t = where(s)
+        def banks_of(u):
+            return range(PACK * units[u][2] // N)
+
+        def product(op, u, b):
+            g, c0, w = units[u]
             bank = psum.tile([P, N], F32, name="bank_" + op)
-            banks[op, s] = bank
-            slots = slice(g * KP + t * P, g * KP + (t + 1) * P)
-            cols = slice(h * N, (h + 1) * N)
-            for k in range(PASSES):
-                nc.tensor.matmul_mx(out=bank[:], lhsT=codes["a", k][:, slots].bitcast(FP8X4), lhsT_scale=scales["a", k][:, slots],
-                                    rhs=codes[op, k][:, cols].bitcast(FP8X4), rhs_scale=scales[op, k][:, cols],
-                                    start=(k == 0), stop=(k == PASSES - 1))
+            banks[op, u, b] = bank
+            cols = slice(c0, c0 + w)
+            for i, t in enumerate(rows_of(u, b)):
+                slots = slice(g * KP + t * P, g * KP + (t + 1) * P)
+                for k in range(PASSES):
+                    nc.tensor.matmul_mx(out=bank[:, i * w:(i + 1) * w],
+                                        lhsT=codes["a", k][:, slots].bitcast(FP8X4), lhsT_scale=scales["a", k][:, slots],
+                                        rhs=codes[op, k][:, cols].bitcast(FP8X4), rhs_scale=scales[op, k][:, cols],
+                                        start=(k == 0), stop=(k == PASSES - 1))
 
-        gates, ys, y_bf = {}, {}, {}
+        def gate(u, b):
+            g, c0, w = units[u]
+            if b % 2 == 0:
+                gates[u, b // 2] = stage.tile([P, 2 * N], F32, name="keep", bufs=4)
+            keep = gates[u, b // 2][:, b % 2 * N:(b % 2 + 1) * N]
+            for i, t in enumerate(rows_of(u, b)):
+                nc.scalar.activation(out=keep[:, i * w:(i + 1) * w], in_=banks["r", u, b][:, i * w:(i + 1) * w], func=ACT.Sigmoid,
+                                     bias=bias_sb[:, g, t:t + 1])
 
-        def gate(s):
-            g, h, t = where(s)
-            keep = stage.tile([P, N], F32, name="keep")
-            gates[s] = keep
-            nc.scalar.activation(out=keep[:], in_=banks["r", s][:], func=ACT.Sigmoid, bias=bias_sb[:, g, t:t + 1])
+        first = {}
 
-        def retain_memory(s):
-            g, h, t = where(s)
-            if t == 0:
-                ys[g, h] = ystage.tile([P, PACK, N], F32, name="y", bufs=6)
-            nc.vector.tensor_tensor(out=ys[g, h][:, t, :], in0=gates[s][:], in1=mem[g][:, t, h * N:(h + 1) * N], op=ALU.mult)
+        def retain_rows(engine, out, u, t0, t1):
+            g, c0, w = units[u]
+            pair_rows = 2 * N // w
+            keep = gates[u, t0 // pair_rows][:].rearrange("p (t m) -> p t m", m=w)[:, t0 % pair_rows:(t1 - 1) % pair_rows + 1, :]
+            engine.tensor_tensor(out=out, in0=keep, in1=mem[g, c0 // N][:, t0:t1, c0 % N:c0 % N + w], op=ALU.mult)
 
-        def add_write(s):
-            g, h, t = where(s)
-            nc.vector.tensor_tensor(out=ys[g, h][:, t, :], in0=banks["c", s][:], in1=ys[g, h][:, t, :], op=ALU.add)
+        def retain_first(u):
+            w = units[u][2]
+            first[u] = ystage.tile([P, N], F32, name="first", bufs=1)
+            retain_rows(nc.gpsimd, first[u][:].rearrange("p (t m) -> p t m", m=w), u, 0, N // w)
 
-        def round_y(u, m0, m1, copy):
-            g, h = divmod(u, HALVES)
-            if u not in y_bf:
-                y_bf[u] = ystage.tile([P, N * PACK], BF16, name="y_bf", align_bytes=64)
-            src = ys[g, h][:, :, m0:m1].rearrange("p t (c i) -> p c t i", i=PACK)
-            dst = y_bf[u][:, m0 * PACK:m1 * PACK].rearrange("p (c i t) -> p c t i", i=PACK, t=PACK)
-            copy(out=dst, in_=src)
+        def retain_memory(u, pair):
+            w = units[u][2]
+            if pair == 0:
+                ys[u] = ystage.tile([P, PACK, w], F32, name="y", bufs=5)
+            t0, t1 = pair * 2 * N // w, (pair + 1) * 2 * N // w
+            if pair == 0 and u in first:
+                t0 = N // w
+            retain_rows(nc.vector, ys[u][:, t0:t1, :], u, t0, t1)
+
+        def add_write(u, b):
+            y = ys[u][:].rearrange("p t m -> p (t m)")[:, b * N:(b + 1) * N]
+            kept = first[u][:] if b == 0 and u in first else y
+            nc.vector.tensor_tensor(out=y, in0=banks["c", u, b][:], in1=kept, op=ALU.add)
+
+        def gpsimd_copy(out, in_):
+            nc.gpsimd.tensor_scalar(out=out, in0=in_, scalar1=1.0, scalar2=0.0, op0=ALU.mult, op1=ALU.add)
+
+        def round_y(u, m0, m1, copy, tile):
+            dst = tile[:].rearrange("p (c i t) -> p c t i", i=PACK, t=PACK)
+            copy(out=dst, in_=ys[u][:, :, m0:m1].rearrange("p t (c i) -> p c t i", i=PACK))
+
+        def new_part(u, m0, m1, name, bufs):
+            tile = ystage.tile([P, (m1 - m0) * PACK], BF16, name=name, align_bytes=64, bufs=bufs)
+            y_bf.setdefault(u, []).append((m0, m1, tile))
+            return tile
+
+        def gpsimd_cols(u):
+            return G_COLS if u < 6 else 0
 
         def quantize_y(u):
-            g, h = divmod(u, HALVES)
-            cols = slice(h * N, (h + 1) * N)
-            nc.vector.quantize_mx(out=y_codes[g][:, cols].bitcast(FP8X4), scales=y_scales[PACK * g:, cols], in_=y_bf[u][:])
+            g, c0, w = units[u]
+            for m0, m1, tile in y_bf[u]:
+                for q0 in range(m0, m1, 256 if m1 - m0 == 384 else N):
+                    q1 = min(m1, q0 + (256 if m1 - m0 == 384 else N))
+                    cols = slice(c0 + q0, c0 + q1)
+                    nc.vector.quantize_mx(out=y_codes[g][:, cols].bitcast(FP8X4), scales=y_scales[PACK * g:, cols],
+                                          in_=tile[:, (q0 - m0) * PACK:(q1 - m0) * PACK])
+            if g == GROUPS - 1:
+                store_words(g, c0, c0 + w)
+            elif c0 + w == WIDTH:
+                store_words(g, 0, WIDTH)
 
-        def store_y(g, h, t0, t1):
+        def store_y(u, t0, t1):
+            g, c0, w = units[u]
             rows = out_0[g * KP:(g + 1) * KP, :].rearrange("(p t) m -> p t m", t=PACK)
-            nc.sync.dma_start(out=rows[:, t0:t1, h * N:(h + 1) * N], in_=ys[g, h][:, t0:t1, :])
+            nc.sync.dma_start(out=rows[:, t0:t1, c0:c0 + w], in_=ys[u][:, t0:t1, :])
 
         def store_words(g, c0, c1):
             words = out_1[g].rearrange("p m t -> p (m t)").bitcast(I32)
             nc.sync.dma_start(out=words[:, c0:c1], in_=y_codes[g][:, c0:c1].bitcast(I32))
 
-        head = [("r", 0, 0), ("r", 0, 1), ("a", 0, 0), ("r", 1, 0), ("r", 1, 1), ("a", 1, 0),
-                ("c", 0, 0), ("c", 0, 1), ("c", 1, 0), ("c", 1, 1)]
-        chunk_at = dict(enumerate(head))
-        chunk_at.update({11: ("a", 0, 1), 12: ("a", 1, 1), 16: ("a", 0, 2), 18: ("a", 1, 2), 23: ("a", 0, 3), 25: ("a", 1, 3)})
-        last_unit = GROUPS * HALVES - 1
-        for tick in range(STEPS + 11):
-            if 0 <= tick - 7 < STEPS:
-                gate(tick - 7)
-            if 0 <= tick - 8 < STEPS:
-                retain_memory(tick - 8)
-            if tick in chunk_at:
-                interleave(chunk_at[tick])
-            s = tick - 10
-            if 0 <= s < STEPS:
-                add_write(s)
-                g, h, t = where(s)
-                if s // PACK == last_unit:
-                    store_y(g, h, t, t + 1)
-                elif t == PACK - 1:
-                    store_y(g, h, 0, PACK)
-            if tick - 1 in chunk_at:
-                quantize(chunk_at[tick - 1])
-            if tick >= 18 and (tick - 18) % PACK == 0:
-                u = (tick - 18) // PACK
-                quantize_y(u)
-                if u % HALVES == 1:
-                    store_words(u // HALVES, 0, WIDTH)
-                elif u == last_unit - 1:
-                    store_words(u // HALVES, 0, N)
-            if tick >= 14:
-                u, q = divmod(tick - 14, PACK)
-                if u < last_unit:
-                    round_y(u, q * PIECE, (q + 1) * PIECE, nc.scalar.copy)
-            if tick == 6:
-                for s in range(2):
-                    product("r", s)
-            if tick == 7:
-                for s in range(2, 3):
-                    product("r", s)
-            if tick == 9:
-                for s in range(2):
-                    product("c", s)
-            if tick >= 10 and tick - 8 < STEPS:
-                product("c", tick - 8)
-            if tick >= 8 and tick - 5 < STEPS:
-                product("r", tick - 5)
+        def share(chunk):
+            interleave(chunk, 0, nc.scalar.copy if chunks.index(chunk) >= 99 else nc.vector.tensor_copy)
+            interleave(chunk, 1, nc.scalar.copy)
 
-        round_y(last_unit, 0, 192, nc.scalar.copy)
-        round_y(last_unit, 192, N, nc.vector.tensor_copy)
-        quantize_y(last_unit)
-        store_words(GROUPS - 1, N, WIDTH)
+        chunks = [("r", 0, 0), ("a", 0, 0), ("r", 1, 0), ("a", 1, 0), ("c", 0, 0), ("c", 1, 0),
+                  ("r", 0, 1), ("r", 1, 1), ("c", 0, 1), ("c", 1, 1)] + [("a", k, g) for g in range(1, GROUPS) for k in range(PASSES)]
+        for n in range(6):
+            if n == 5:
+                for b in range(0):
+                    gate(0, b)
+            share(chunks[n])
+            if n:
+                quantize(chunks[n - 1])
+            if n == 4:
+                for b in banks_of(0):
+                    product("r", 0, b)
+        quantize(chunks[5])
+        for b in range(0, PACK):
+            gate(0, b)
+        plan = [chunks[6:10], chunks[10:12], chunks[12:14], chunks[14:15], chunks[15:16]]
+
+        for u in range(len(units)):
+            todo = plan[u] if u < len(plan) else []
+            late_write = todo[:1] == [("c", 1, 1)]
+            late_logits = u < 2
+            for b in range(PACK):
+                if u + 1 <= last and b in banks_of(u + 1) and not late_logits:
+                    product("r", u + 1, b)
+                if b in banks_of(u) and not late_write:
+                    product("c", u, b)
+            retain_memory(u, 0)
+            for n, chunk in enumerate(todo):
+                share(chunk)
+                if n == 0:
+                    retain_memory(u, 1)
+                else:
+                    quantize(todo[n - 1])
+                    if u == 0 and n == 2:
+                        for b in banks_of(1):
+                            product("r", 1, b)
+                    if late_write and n == 1:
+                        for b in banks_of(u):
+                            product("c", u, b)
+            if not todo and len(banks_of(u)) == PACK:
+                retain_memory(u, 1)
+            if u < last and not late_logits:
+                for b in banks_of(u + 1):
+                    gate(u + 1, b)
+            if u >= 1:
+                w = units[u - 1][2]
+                round_y(u - 1, gpsimd_cols(u - 1), w, nc.scalar.copy, new_part(u - 1, gpsimd_cols(u - 1), w, "y_bf", 2))
+            if todo:
+                quantize(todo[-1])
+            if late_logits and u:
+                for b in banks_of(u + 1):
+                    product("r", u + 1, b)
+            if u >= 2:
+                quantize_y(u - 2)
+            if u >= 1 and gpsimd_cols(u - 1):
+                round_y(u - 1, 0, G_COLS, gpsimd_copy, new_part(u - 1, 0, G_COLS, "y_bf_g", 1))
+            for b in banks_of(u):
+                add_write(u, b)
+                if b == 0 and 99 <= u + 1 <= last:
+                    retain_first(u + 1)
+                if u >= last - 2:
+                    store_y(u, rows_of(u, b)[0], rows_of(u, b)[-1] + 1)
+            if u < last - 2:
+                store_y(u, 0, PACK)
+            if late_logits:
+                for b in banks_of(u + 1):
+                    gate(u + 1, b)
+
+        tile = new_part(last, 0, units[last][2], "y_bf", 2)
+        round_y(last, 0, 64, nc.scalar.copy, tile[:, :64 * PACK])
+        quantize_y(last - 1)
+        round_y(last, 64, units[last][2], nc.vector.tensor_copy, tile[:, 64 * PACK:])
+        quantize_y(last)
         for q in range(PACK):
-            queue = nc.sync if q % 2 == 0 else nc.scalar
-            queue.dma_start(out=out_2[:, PACK * q:PACK * (q + 1), :].bitcast(I32),
-                            in_=y_scales[32 * q:32 * q + PACK * GROUPS, :].bitcast(I32))
+            nc.scalar.dma_start(out=out_2[:, PACK * q:PACK * (q + 1), :].bitcast(I32),
+                                in_=y_scales[32 * q:32 * q + PACK * GROUPS, :].bitcast(I32))

@@ -22,8 +22,9 @@ GROUPS = SLOTS // KP
 N = 512
 HALVES = WIDTH // N
 STEPS = GROUPS * HALVES * PACK
-V_COLS = 224
-G_COLS = 0
+V_COLS = 256
+G_RETAIN = 384
+G_COLS = 128
 
 
 def tile_gated_memory_write_g2_kernel(tc, addr, content, retain, memory, bias, out_0, out_1, out_2):
@@ -142,35 +143,30 @@ def tile_gated_memory_write_g2_kernel(tc, addr, content, retain, memory, bias, o
                 nc.scalar.activation(out=keep[:, i * w:(i + 1) * w], in_=banks["r", u, b][:, i * w:(i + 1) * w], func=ACT.Sigmoid,
                                      bias=bias_sb[:, g, t:t + 1])
 
-        first = {}
-
-        def retain_rows(engine, out, u, t0, t1):
+        def retain_rows(engine, u, t0, t1, m0, m1):
             g, c0, w = units[u]
+            if u not in ys:
+                ys[u] = ystage.tile([P, PACK, w], F32, name="y", bufs=5)
             pair_rows = 2 * N // w
-            keep = gates[u, t0 // pair_rows][:].rearrange("p (t m) -> p t m", m=w)[:, t0 % pair_rows:(t1 - 1) % pair_rows + 1, :]
-            engine.tensor_tensor(out=out, in0=keep, in1=mem[g, c0 // N][:, t0:t1, c0 % N:c0 % N + w], op=ALU.mult)
-
-        def retain_first(u):
-            w = units[u][2]
-            first[u] = ystage.tile([P, N], F32, name="first", bufs=1)
-            retain_rows(nc.gpsimd, first[u][:].rearrange("p (t m) -> p t m", m=w), u, 0, N // w)
+            keep = gates[u, t0 // pair_rows][:].rearrange("p (t m) -> p t m", m=w)[:, t0 % pair_rows:(t1 - 1) % pair_rows + 1, m0:m1]
+            engine.tensor_tensor(out=ys[u][:, t0:t1, m0:m1], in0=keep, in1=mem[g, c0 // N][:, t0:t1, c0 % N + m0:c0 % N + m1], op=ALU.mult)
 
         def retain_memory(u, pair):
             w = units[u][2]
-            if pair == 0:
-                ys[u] = ystage.tile([P, PACK, w], F32, name="y", bufs=5)
             t0, t1 = pair * 2 * N // w, (pair + 1) * 2 * N // w
-            if pair == 0 and u in first:
-                t0 = N // w
-            retain_rows(nc.vector, ys[u][:, t0:t1, :], u, t0, t1)
+            if pair == 0 and u in ys:
+                t0 = 1
+                if G_RETAIN < w:
+                    retain_rows(nc.vector, u, 0, 1, G_RETAIN, w)
+            retain_rows(nc.vector, u, t0, t1, 0, w)
 
         def add_write(u, b):
             y = ys[u][:].rearrange("p t m -> p (t m)")[:, b * N:(b + 1) * N]
-            kept = first[u][:] if b == 0 and u in first else y
-            nc.vector.tensor_tensor(out=y, in0=banks["c", u, b][:], in1=kept, op=ALU.add)
+            nc.vector.tensor_tensor(out=y, in0=banks["c", u, b][:], in1=y, op=ALU.add)
 
-        def gpsimd_copy(out, in_):
-            nc.gpsimd.tensor_scalar(out=out, in0=in_, scalar1=1.0, scalar2=0.0, op0=ALU.mult, op1=ALU.add)
+        def round_y_gpsimd(u, tile):
+            nc.gpsimd.tensor_scalar(out=tile[:].rearrange("p (m t) -> p m t", t=PACK), in0=ys[u][:, :, :G_COLS].rearrange("p t m -> p m t"),
+                                    scalar1=1.0, scalar2=0.0, op0=ALU.mult, op1=ALU.add)
 
         def round_y(u, m0, m1, copy, tile):
             dst = tile[:].rearrange("p (c i t) -> p c t i", i=PACK, t=PACK)
@@ -182,7 +178,7 @@ def tile_gated_memory_write_g2_kernel(tc, addr, content, retain, memory, bias, o
             return tile
 
         def gpsimd_cols(u):
-            return G_COLS if u < 6 else 0
+            return G_COLS if u < 7 else 0
 
         def quantize_y(u):
             g, c0, w = units[u]
@@ -240,7 +236,8 @@ def tile_gated_memory_write_g2_kernel(tc, addr, content, retain, memory, bias, o
             for n, chunk in enumerate(todo):
                 share(chunk)
                 if n == 0:
-                    retain_memory(u, 1)
+                    if u != 1:
+                        retain_memory(u, 1)
                 else:
                     quantize(todo[n - 1])
                     if u == 0 and n == 2:
@@ -262,14 +259,20 @@ def tile_gated_memory_write_g2_kernel(tc, addr, content, retain, memory, bias, o
             if late_logits and u:
                 for b in banks_of(u + 1):
                     product("r", u + 1, b)
+            if u == 1:
+                retain_memory(u, 1)
             if u >= 2:
                 quantize_y(u - 2)
             if u >= 1 and gpsimd_cols(u - 1):
-                round_y(u - 1, 0, G_COLS, gpsimd_copy, new_part(u - 1, 0, G_COLS, "y_bf_g", 1))
+                tile = new_part(u - 1, 0, G_COLS, "y_bf_g", 1)
+                if u == 1:
+                    round_y(u - 1, 0, G_COLS, nc.scalar.copy, tile)
+                else:
+                    round_y_gpsimd(u - 1, tile)
             for b in banks_of(u):
                 add_write(u, b)
-                if b == 0 and 99 <= u + 1 <= last:
-                    retain_first(u + 1)
+                if b == 0 and 3 <= u + 1 <= 7:
+                    retain_rows(nc.gpsimd, u + 1, 0, 1, 0, min(G_RETAIN, units[u + 1][2]))
                 if u >= last - 2:
                     store_y(u, rows_of(u, b)[0], rows_of(u, b)[-1] + 1)
             if u < last - 2:
@@ -279,10 +282,11 @@ def tile_gated_memory_write_g2_kernel(tc, addr, content, retain, memory, bias, o
                     gate(u + 1, b)
 
         tile = new_part(last, 0, units[last][2], "y_bf", 2)
-        round_y(last, 0, 64, nc.scalar.copy, tile[:, :64 * PACK])
+        round_y(last, 0, 96, nc.scalar.copy, tile[:, :96 * PACK])
         quantize_y(last - 1)
-        round_y(last, 64, units[last][2], nc.vector.tensor_copy, tile[:, 64 * PACK:])
+        round_y(last, 96, units[last][2], nc.vector.tensor_copy, tile[:, 96 * PACK:])
         quantize_y(last)
         for q in range(PACK):
-            nc.scalar.dma_start(out=out_2[:, PACK * q:PACK * (q + 1), :].bitcast(I32),
-                                in_=y_scales[32 * q:32 * q + PACK * GROUPS, :].bitcast(I32))
+            queue = nc.sync if q == 0 else nc.scalar
+            queue.dma_start(out=out_2[:, PACK * q:PACK * (q + 1), :].bitcast(I32),
+                            in_=y_scales[32 * q:32 * q + PACK * GROUPS, :].bitcast(I32))

@@ -22,9 +22,9 @@ GROUPS = SLOTS // KP
 N = 512
 HALVES = WIDTH // N
 STEPS = GROUPS * HALVES * PACK
-V_COLS = 256
-G_RETAIN = 384
-G_COLS = 128
+V_COLS = 240
+G_RETAIN = 512
+G_COLS = 64
 
 
 def tile_gated_memory_write_g2_kernel(tc, addr, content, retain, memory, bias, out_0, out_1, out_2):
@@ -79,11 +79,11 @@ def tile_gated_memory_write_g2_kernel(tc, addr, content, retain, memory, bias, o
         load("r", 1, 1, 2)
         load("c", 0, 1, 2)
         load("c", 1, 1, 2)
-        load_mem(0, 1, 2)
         load("a", 0, 1, 2)
+        load_mem(0, 1, 2)
         load("a", 1, 1, 2)
-        load_mem(1, 0, 2)
         load("a", 0, 2, 4)
+        load_mem(1, 0, 2)
         load("a", 1, 2, 4)
         load_mem(2, 0, 2)
         load_mem(3, 0, 2)
@@ -93,7 +93,9 @@ def tile_gated_memory_write_g2_kernel(tc, addr, content, retain, memory, bias, o
         def interleave(chunk, half, copy):
             op, k, c = chunk
             if chunk not in grouped:
-                grouped[chunk] = stage.tile([P, N * PACK], BF16, name="grouped", align_bytes=64)
+                n = len(grouped)
+                slot = n % 3 if n < 10 else (0, 1, 1, 2, 0, 1)[n - 10]
+                grouped[chunk] = stage.tile([P, N * PACK], BF16, name="grouped%d" % slot, align_bytes=64, bufs=1)
             src, dst = raw[chunk], grouped[chunk][:]
             if op == "a":
                 part = slice(2 * half, 2 * half + 2)
@@ -178,7 +180,7 @@ def tile_gated_memory_write_g2_kernel(tc, addr, content, retain, memory, bias, o
             return tile
 
         def gpsimd_cols(u):
-            return G_COLS if u < 7 else 0
+            return G_COLS if u < 6 else 0
 
         def quantize_y(u):
             g, c0, w = units[u]
@@ -202,7 +204,16 @@ def tile_gated_memory_write_g2_kernel(tc, addr, content, retain, memory, bias, o
             words = out_1[g].rearrange("p m t -> p (m t)").bitcast(I32)
             nc.sync.dma_start(out=words[:, c0:c1], in_=y_codes[g][:, c0:c1].bitcast(I32))
 
+        def interleave_gpsimd(chunk):
+            def copy(out, in_):
+                nc.gpsimd.tensor_scalar(out=out.rearrange("p m j t -> p t m j"), in0=in_.rearrange("p m j t -> p t m j"),
+                                        scalar1=1.0, scalar2=0.0, op0=ALU.mult, op1=ALU.add)
+            interleave(chunk, 0, copy)
+
         def share(chunk):
+            if chunk in grouped:
+                interleave(chunk, 1, nc.scalar.copy)
+                return
             interleave(chunk, 0, nc.scalar.copy if chunks.index(chunk) >= 99 else nc.vector.tensor_copy)
             interleave(chunk, 1, nc.scalar.copy)
 
@@ -210,16 +221,20 @@ def tile_gated_memory_write_g2_kernel(tc, addr, content, retain, memory, bias, o
                   ("r", 0, 1), ("r", 1, 1), ("c", 0, 1), ("c", 1, 1)] + [("a", k, g) for g in range(1, GROUPS) for k in range(PASSES)]
         for n in range(6):
             if n == 5:
-                for b in range(0):
+                for b in range(2):
                     gate(0, b)
-            share(chunks[n])
+            if n == 5:
+                interleave(chunks[n], 0, nc.vector.tensor_copy)
+                interleave(chunks[n], 1, nc.vector.tensor_copy)
+            else:
+                share(chunks[n])
             if n:
                 quantize(chunks[n - 1])
             if n == 4:
                 for b in banks_of(0):
                     product("r", 0, b)
         quantize(chunks[5])
-        for b in range(0, PACK):
+        for b in range(2, PACK):
             gate(0, b)
         plan = [chunks[6:10], chunks[10:12], chunks[12:14], chunks[14:15], chunks[15:16]]
 
@@ -227,9 +242,10 @@ def tile_gated_memory_write_g2_kernel(tc, addr, content, retain, memory, bias, o
             todo = plan[u] if u < len(plan) else []
             late_write = todo[:1] == [("c", 1, 1)]
             late_logits = u < 2
+            ahead = [(v, b) for v in range(u + 1, last + 1) for b in banks_of(v)][:PACK] if u != last - 1 else []
             for b in range(PACK):
-                if u + 1 <= last and b in banks_of(u + 1) and not late_logits:
-                    product("r", u + 1, b)
+                if b < len(ahead) and not late_logits:
+                    product("r", *ahead[b])
                 if b in banks_of(u) and not late_write:
                     product("c", u, b)
             retain_memory(u, 0)
@@ -248,12 +264,9 @@ def tile_gated_memory_write_g2_kernel(tc, addr, content, retain, memory, bias, o
                             product("c", u, b)
             if not todo and len(banks_of(u)) == PACK:
                 retain_memory(u, 1)
-            if u < last and not late_logits:
-                for b in banks_of(u + 1):
-                    gate(u + 1, b)
-            if u >= 1:
-                w = units[u - 1][2]
-                round_y(u - 1, gpsimd_cols(u - 1), w, nc.scalar.copy, new_part(u - 1, gpsimd_cols(u - 1), w, "y_bf", 2))
+            if not late_logits:
+                for v, b in ahead:
+                    gate(v, b)
             if todo:
                 quantize(todo[-1])
             if late_logits and u:
@@ -263,16 +276,20 @@ def tile_gated_memory_write_g2_kernel(tc, addr, content, retain, memory, bias, o
                 retain_memory(u, 1)
             if u >= 2:
                 quantize_y(u - 2)
-            if u >= 1 and gpsimd_cols(u - 1):
-                tile = new_part(u - 1, 0, G_COLS, "y_bf_g", 1)
-                if u == 1:
-                    round_y(u - 1, 0, G_COLS, nc.scalar.copy, tile)
-                else:
-                    round_y_gpsimd(u - 1, tile)
+            if u >= 1:
+                w = units[u - 1][2]
+                tile = new_part(u - 1, 0, w, "y_bf_g" if u - 1 < 6 else "y_bf%d" % u, 1)
+                cut = G_COLS if 1 <= u - 1 < 6 else 0
+                if cut:
+                    round_y_gpsimd(u - 1, tile[:, :cut * PACK])
+                round_y(u - 1, cut, w, nc.scalar.copy, tile[:, cut * PACK:])
+            if u < 2:
+                interleave_gpsimd(plan[u + 1][0])
             for b in banks_of(u):
                 add_write(u, b)
-                if b == 0 and 3 <= u + 1 <= 7:
-                    retain_rows(nc.gpsimd, u + 1, 0, 1, 0, min(G_RETAIN, units[u + 1][2]))
+                if b == 0 and u >= 2:
+                    for v in sorted(set(v for v, bank in ahead))[:2]:
+                        retain_rows(nc.gpsimd, v, 0, 1, 0, min(G_RETAIN, units[v][2]))
                 if u >= last - 2:
                     store_y(u, rows_of(u, b)[0], rows_of(u, b)[-1] + 1)
             if u < last - 2:
@@ -281,7 +298,7 @@ def tile_gated_memory_write_g2_kernel(tc, addr, content, retain, memory, bias, o
                 for b in banks_of(u + 1):
                     gate(u + 1, b)
 
-        tile = new_part(last, 0, units[last][2], "y_bf", 2)
+        tile = new_part(last, 0, units[last][2], "y_bf_last", 1)
         round_y(last, 0, 96, nc.scalar.copy, tile[:, :96 * PACK])
         quantize_y(last - 1)
         round_y(last, 96, units[last][2], nc.vector.tensor_copy, tile[:, 96 * PACK:])

@@ -102,10 +102,10 @@ def tile_gated_memory_write_g2_kernel(tc, addr, content, retain, memory, bias, o
                 copy(out=dst.rearrange("p (t m j) -> p m j t", t=PACK, j=PACK)[:, :, :, part],
                      in_=src.rearrange("p j (m t) -> p m j t", t=PACK)[:, :, :, part])
             else:
-                cut = (V_COLS if c else N // 2) // PACK
-                part = slice(cut, N // PACK) if half else slice(0, cut)
-                copy(out=dst.rearrange("p (c i j) -> p c j i", i=PACK, j=PACK)[:, part],
-                     in_=src.rearrange("p j (c i) -> p c j i", i=PACK)[:, part])
+                cut = (V_COLS if c else N // 2) // 2
+                part = slice(cut, N // 2) if half else slice(0, cut)
+                copy(out=dst.rearrange("p (c i j) -> p c j i", i=2, j=PACK)[:, part],
+                     in_=src.rearrange("p j (c i) -> p c j i", i=2)[:, part])
 
         def quantize(chunk):
             op, k, c = chunk
@@ -171,8 +171,8 @@ def tile_gated_memory_write_g2_kernel(tc, addr, content, retain, memory, bias, o
                                     scalar1=1.0, scalar2=0.0, op0=ALU.mult, op1=ALU.add)
 
         def round_y(u, m0, m1, copy, tile):
-            dst = tile[:].rearrange("p (c i t) -> p c t i", i=PACK, t=PACK)
-            copy(out=dst, in_=ys[u][:, :, m0:m1].rearrange("p t (c i) -> p c t i", i=PACK))
+            dst = tile[:].rearrange("p (c i t) -> p c t i", i=2, t=PACK)
+            copy(out=dst, in_=ys[u][:, :, m0:m1].rearrange("p t (c i) -> p c t i", i=2))
 
         def new_part(u, m0, m1, name, bufs):
             tile = ystage.tile([P, (m1 - m0) * PACK], BF16, name=name, align_bytes=64, bufs=bufs)

from contextlib import ExitStack

import concourse.mybir as mybir

T, SLOTS, WIDTH = 1024, 2048, 1024
FLOPS = 2 * 2 * T * SLOTS * WIDTH

F32 = mybir.dt.float32
BF16 = mybir.dt.bfloat16
I32 = mybir.dt.int32
U32 = mybir.dt.uint32
U8 = mybir.dt.uint8
FP8X4 = mybir.dt.float8_e4m3fn_x4
ACT = mybir.ActivationFunctionType
ALU = mybir.AluOpType

P = 128
PACK = 4
KP = P * PACK
PASSES = T // KP
GROUPS = SLOTS // KP
N = 512
HALVES = WIDTH // N
STEPS = GROUPS * HALVES * PACK
V_COLS = 240
G_RETAIN = 512
G_COLS = 64


def tile_gated_memory_write_g2_kernel(tc, addr, content, retain, memory, bias, out_0, out_1, out_2):
    nc = tc.nc
    with ExitStack() as ctx:
        keep_pool = ctx.enter_context(tc.tile_pool(name="resident", bufs=1))
        stage = ctx.enter_context(tc.tile_pool(name="stage", bufs=3))
        ystage = ctx.enter_context(tc.tile_pool(name="ystage", bufs=2))
        psum = ctx.enter_context(tc.psum_pool(name="psum", bufs=4))
        ctx.enter_context(tc.manual_schedule())

        source = {"a": addr, "c": content, "r": retain}
        raw, codes, scales = {}, {}, {}
        for op in "rac":
            width = source[op].shape[1]
            for k in range(PASSES):
                codes[op, k] = keep_pool.tile([P, width], U32, name="codes_%s%d" % (op, k), align_bytes=64)
                scales[op, k] = keep_pool.tile([P, width], U8, name="scales_%s%d" % (op, k), align_bytes=64)
        mem = {}
        y_codes = [keep_pool.tile([P, WIDTH], U32, name="y_codes%d" % g, align_bytes=64) for g in range(GROUPS)]
        y_scales = keep_pool.tile([P, WIDTH], U8, name="y_scales", align_bytes=64)
        bias_sb = keep_pool.tile([P, GROUPS, PACK], BF16, name="bias_sb", align_bytes=64)
        warm_in = keep_pool.tile([P, 1], F32, name="warm_in")
        warm_out = keep_pool.tile([P, 1], F32, name="warm_out")

        def load(op, k, c0, c1):
            rows = source[op][k * KP:(k + 1) * KP, c0 * N:c1 * N]
            dst = keep_pool.tile([P, PACK, (c1 - c0) * N], BF16, name="raw_%s%d%d" % (op, k, c0), align_bytes=64)
            nc.sync.dma_start(out=dst[:], in_=rows.rearrange("(p j) w -> p j w", j=PACK))
            for c in range(c0, c1):
                raw[op, k, c] = dst[:, :, (c - c0) * N:(c - c0 + 1) * N]

        def load_mem(g, h0, h1):
            rows = memory[g * KP:(g + 1) * KP, h0 * N:h1 * N]
            dst = keep_pool.tile([P, PACK, (h1 - h0) * N], BF16, name="mem%d%d" % (g, h0), align_bytes=64)
            nc.sync.dma_start(out=dst[:], in_=rows.rearrange("(p t) w -> p t w", t=PACK))
            for h in range(h0, h1):
                mem[g, h] = dst[:, :, (h - h0) * N:(h - h0 + 1) * N]

        nc.vector.memset(warm_in[:], 0.0)
        nc.scalar.activation(out=warm_out[:], in_=warm_in[:], func=ACT.Sigmoid)

        load("r", 0, 0, 1)
        load("a", 0, 0, 1)
        load("r", 1, 0, 1)
        load("a", 1, 0, 1)
        load("c", 0, 0, 1)
        load("c", 1, 0, 1)
        nc.sync.dma_start(out=bias_sb[:], in_=bias.rearrange("(g p t) -> p g t", p=P, t=PACK))
        load_mem(0, 0, 1)
        load("r", 0, 1, 2)
        load("r", 1, 1, 2)
        load("c", 0, 1, 2)
        load("c", 1, 1, 2)
        load("a", 0, 1, 2)
        load_mem(0, 1, 2)
        load("a", 1, 1, 2)
        load("a", 0, 2, 4)
        load_mem(1, 0, 2)
        load("a", 1, 2, 4)
        load_mem(2, 0, 2)
        load_mem(3, 0, 2)

        grouped = {}

        def interleave(chunk, half, copy):
            op, k, c = chunk
            if chunk not in grouped:
                n = len(grouped)
                slot = n % 3 if n < 10 else (0, 1, 1, 2, 0, 1)[n - 10]
                grouped[chunk] = stage.tile([P, N * PACK], BF16, name="grouped%d" % slot, align_bytes=64, bufs=1)
            src, dst = raw[chunk], grouped[chunk][:]
            if op == "a":
                part = slice(2 * half, 2 * half + 2)
                copy(out=dst.rearrange("p (t m j) -> p m j t", t=PACK, j=PACK)[:, :, :, part],
                     in_=src.rearrange("p j (m t) -> p m j t", t=PACK)[:, :, :, part])
            else:
                cut = (V_COLS if c else N // 2) // 2
                part = slice(cut, N // 2) if half else slice(0, cut)
                copy(out=dst.rearrange("p (c i j) -> p c j i", i=2, j=PACK)[:, part],
                     in_=src.rearrange("p j (c i) -> p c j i", i=2)[:, part])

        def quantize(chunk):
            op, k, c = chunk
            cols = slice(c * N, (c + 1) * N)
            nc.vector.quantize_mx(out=codes[op, k][:, cols].bitcast(FP8X4), scales=scales[op, k][:, cols], in_=grouped[chunk][:])

        units = [(g, h * N, N) for g in range(GROUPS) for h in range(HALVES)][:-1] + [(3, 512, 256), (3, 768, 256)]
        last = len(units) - 1
        banks, gates, ys, y_bf = {}, {}, {}, {}

        def rows_of(u, b):
            per_bank = N // units[u][2]
            return range(b * per_bank, (b + 1) * per_bank)

        def banks_of(u):
            return range(PACK * units[u][2] // N)

        def product(op, u, b):
            g, c0, w = units[u]
            bank = psum.tile([P, N], F32, name="bank_" + op)
            banks[op, u, b] = bank
            cols = slice(c0, c0 + w)
            for i, t in enumerate(rows_of(u, b)):
                slots = slice(g * KP + t * P, g * KP + (t + 1) * P)
                for k in range(PASSES):
                    nc.tensor.matmul_mx(out=bank[:, i * w:(i + 1) * w],
                                        lhsT=codes["a", k][:, slots].bitcast(FP8X4), lhsT_scale=scales["a", k][:, slots],
                                        rhs=codes[op, k][:, cols].bitcast(FP8X4), rhs_scale=scales[op, k][:, cols],
                                        start=(k == 0), stop=(k == PASSES - 1))

        def gate(u, b):
            g, c0, w = units[u]
            if b % 2 == 0:
                gates[u, b // 2] = stage.tile([P, 2 * N], F32, name="keep", bufs=4)
            keep = gates[u, b // 2][:, b % 2 * N:(b % 2 + 1) * N]
            for i, t in enumerate(rows_of(u, b)):
                nc.scalar.activation(out=keep[:, i * w:(i + 1) * w], in_=banks["r", u, b][:, i * w:(i + 1) * w], func=ACT.Sigmoid,
                                     bias=bias_sb[:, g, t:t + 1])

        def retain_rows(engine, u, t0, t1, m0, m1):
            g, c0, w = units[u]
            if u not in ys:
                ys[u] = ystage.tile([P, PACK, w], F32, name="y", bufs=5)
            pair_rows = 2 * N // w
            keep = gates[u, t0 // pair_rows][:].rearrange("p (t m) -> p t m", m=w)[:, t0 % pair_rows:(t1 - 1) % pair_rows + 1, m0:m1]
            engine.tensor_tensor(out=ys[u][:, t0:t1, m0:m1], in0=keep, in1=mem[g, c0 // N][:, t0:t1, c0 % N + m0:c0 % N + m1], op=ALU.mult)

        def retain_memory(u, pair):
            w = units[u][2]
            t0, t1 = pair * 2 * N // w, (pair + 1) * 2 * N // w
            if pair == 0 and u in ys:
                t0 = 1
                if G_RETAIN < w:
                    retain_rows(nc.vector, u, 0, 1, G_RETAIN, w)
            retain_rows(nc.vector, u, t0, t1, 0, w)

        def add_write(u, b):
            y = ys[u][:].rearrange("p t m -> p (t m)")[:, b * N:(b + 1) * N]
            nc.vector.tensor_tensor(out=y, in0=banks["c", u, b][:], in1=y, op=ALU.add)

        def round_y_gpsimd(u, tile):
            nc.gpsimd.tensor_scalar(out=tile[:].rearrange("p (m t) -> p m t", t=PACK), in0=ys[u][:, :, :G_COLS].rearrange("p t m -> p m t"),
                                    scalar1=1.0, scalar2=0.0, op0=ALU.mult, op1=ALU.add)

        def round_y(u, m0, m1, copy, tile):
            dst = tile[:].rearrange("p (c i t) -> p c t i", i=2, t=PACK)
            copy(out=dst, in_=ys[u][:, :, m0:m1].rearrange("p t (c i) -> p c t i", i=2))

        def new_part(u, m0, m1, name, bufs):
            tile = ystage.tile([P, (m1 - m0) * PACK], BF16, name=name, align_bytes=64, bufs=bufs)
            y_bf.setdefault(u, []).append((m0, m1, tile))
            return tile

        def gpsimd_cols(u):
            return G_COLS if u < 6 else 0

        def quantize_y(u):
            g, c0, w = units[u]
            for m0, m1, tile in y_bf[u]:
                for q0 in range(m0, m1, 256 if m1 - m0 == 384 else N):
                    q1 = min(m1, q0 + (256 if m1 - m0 == 384 else N))
                    cols = slice(c0 + q0, c0 + q1)
                    nc.vector.quantize_mx(out=y_codes[g][:, cols].bitcast(FP8X4), scales=y_scales[PACK * g:, cols],
                                          in_=tile[:, (q0 - m0) * PACK:(q1 - m0) * PACK])
            if g == GROUPS - 1:
                store_words(g, c0, c0 + w)
            elif c0 + w == WIDTH:
                store_words(g, 0, WIDTH)

        def store_y(u, t0, t1):
            g, c0, w = units[u]
            rows = out_0[g * KP:(g + 1) * KP, :].rearrange("(p t) m -> p t m", t=PACK)
            nc.sync.dma_start(out=rows[:, t0:t1, c0:c0 + w], in_=ys[u][:, t0:t1, :])

        def store_words(g, c0, c1):
            words = out_1[g].rearrange("p m t -> p (m t)").bitcast(I32)
            nc.sync.dma_start(out=words[:, c0:c1], in_=y_codes[g][:, c0:c1].bitcast(I32))

        def interleave_gpsimd(chunk):
            def copy(out, in_):
                nc.gpsimd.tensor_scalar(out=out.rearrange("p m j t -> p t m j"), in0=in_.rearrange("p m j t -> p t m j"),
                                        scalar1=1.0, scalar2=0.0, op0=ALU.mult, op1=ALU.add)
            interleave(chunk, 0, copy)

        def share(chunk):
            if chunk in grouped:
                interleave(chunk, 1, nc.scalar.copy)
                return
            interleave(chunk, 0, nc.scalar.copy if chunks.index(chunk) >= 99 else nc.vector.tensor_copy)
            interleave(chunk, 1, nc.scalar.copy)

        chunks = [("r", 0, 0), ("a", 0, 0), ("r", 1, 0), ("a", 1, 0), ("c", 0, 0), ("c", 1, 0),
                  ("r", 0, 1), ("r", 1, 1), ("c", 0, 1), ("c", 1, 1)] + [("a", k, g) for g in range(1, GROUPS) for k in range(PASSES)]
        for n in range(6):
            if n == 5:
                for b in range(2):
                    gate(0, b)
            if n == 5:
                interleave(chunks[n], 0, nc.vector.tensor_copy)
                interleave(chunks[n], 1, nc.vector.tensor_copy)
            else:
                share(chunks[n])
            if n:
                quantize(chunks[n - 1])
            if n == 4:
                for b in banks_of(0):
                    product("r", 0, b)
        quantize(chunks[5])
        for b in range(2, PACK):
            gate(0, b)
        plan = [chunks[6:10], chunks[10:12], chunks[12:14], chunks[14:15], chunks[15:16]]

        for u in range(len(units)):
            todo = plan[u] if u < len(plan) else []
            late_write = todo[:1] == [("c", 1, 1)]
            late_logits = u < 2
            ahead = [(v, b) for v in range(u + 1, last + 1) for b in banks_of(v)][:PACK] if u != last - 1 else []
            for b in range(PACK):
                if b < len(ahead) and not late_logits:
                    product("r", *ahead[b])
                if b in banks_of(u) and not late_write:
                    product("c", u, b)
            retain_memory(u, 0)
            for n, chunk in enumerate(todo):
                share(chunk)
                if n == 0:
                    if u != 1:
                        retain_memory(u, 1)
                else:
                    quantize(todo[n - 1])
                    if u == 0 and n == 2:
                        for b in banks_of(1):
                            product("r", 1, b)
                    if late_write and n == 1:
                        for b in banks_of(u):
                            product("c", u, b)
            if not todo and len(banks_of(u)) == PACK:
                retain_memory(u, 1)
            if not late_logits:
                for v, b in ahead:
                    gate(v, b)
            if todo:
                quantize(todo[-1])
            if late_logits and u:
                for b in banks_of(u + 1):
                    product("r", u + 1, b)
            if u == 1:
                retain_memory(u, 1)
            if u >= 2:
                quantize_y(u - 2)
            if u >= 1:
                w = units[u - 1][2]
                tile = new_part(u - 1, 0, w, "y_bf_g" if u - 1 < 6 else "y_bf%d" % u, 1)
                cut = G_COLS if 1 <= u - 1 < 6 else 0
                if cut:
                    round_y_gpsimd(u - 1, tile[:, :cut * PACK])
                round_y(u - 1, cut, w, nc.scalar.copy, tile[:, cut * PACK:])
            if u < 2:
                interleave_gpsimd(plan[u + 1][0])
            for b in banks_of(u):
                add_write(u, b)
                if b == 0 and u >= 2:
                    for v in sorted(set(v for v, bank in ahead))[:2]:
                        retain_rows(nc.gpsimd, v, 0, 1, 0, min(G_RETAIN, units[v][2]))
                if u >= last - 2:
                    store_y(u, rows_of(u, b)[0], rows_of(u, b)[-1] + 1)
            if u < last - 2:
                store_y(u, 0, PACK)
            if late_logits:
                for b in banks_of(u + 1):
                    gate(u + 1, b)

        tile = new_part(last, 0, units[last][2], "y_bf_last", 1)
        round_y(last, 0, 96, nc.scalar.copy, tile[:, :96 * PACK])
        quantize_y(last - 1)
        round_y(last, 96, units[last][2], nc.vector.tensor_copy, tile[:, 96 * PACK:])
        quantize_y(last)
        for q in range(PACK):
            queue = nc.sync if q == 0 else nc.scalar
            queue.dma_start(out=out_2[:, PACK * q:PACK * (q + 1), :].bitcast(I32),
                            in_=y_scales[32 * q:32 * q + PACK * GROUPS, :].bitcast(I32))
